import numpy as np, ml_dtypes
CORES = [71,199,95,223,103,231,111,239,119,247,127,255]
N = 12
GR, GC = 2, 6
L, KA, KB, F = 6, 1, 3, 512
def setup_inputs(rng):
    return {"a": rng.standard_normal((N, 128, KA * 128), dtype=np.float32).astype(ml_dtypes.bfloat16), "b": rng.standard_normal((N, 128, KB * F), dtype=np.float32).astype(ml_dtypes.bfloat16)}
def reference(a, b):
    A, B = a.astype(np.float64), b.astype(np.float64)
    y = np.zeros((N, 128, F))
    for i in range(GR):
        for j in range(GC):
            for k in range(L):
                At = A[i * GC + k // KA][:, 128 * (k % KA):128 * (k % KA) + 128]
                Bt = B[(k // KB) * GC + j][:, F * (k % KB):F * (k % KB) + F]
                y[i * GC + j] += At.T @ Bt
    return {"y": y.astype(ml_dtypes.bfloat16 if a.dtype != np.float64 else np.float64)}

@@ -1,0 +1,111 @@
+from concourse.bass import DstId, RemoteDMATransfer
+
+GR, GC, KB, F, P = 2, 6, 3, 512, 128
+HF = F // 2
+NB = KB * KB
+
+SCRATCH = {
+    "ad": ("dram", [GC * P, P], "bfloat16"),
+    "asb": ("sbuf", [P, GC * P], "bfloat16"),
+    "bown": ("sbuf", [P, KB * F], "bfloat16"),
+    "bpeer": ("sbuf", [P, KB * F], "bfloat16"),
+    "ysb": ("sbuf", [P, F], "bfloat16"),
+    "acc0": ("psum", [P, F], "float32"),
+    "acc1": ("psum", [P, F], "float32"),
+}
+SEMAPHORES = ["a_st", "b_ld", "a_in0", "a_in1", "a_sb0", "a_sb1", "b_in", "sent",
+              "mm0", "mm1", "cp0", "cp1", "st0", "st1"]
+
+
+def _engines(mask):
+    return bin(mask).count("1")
+
+
+def _row_peers(T, rank):
+    row, col = rank // GC, rank % GC
+    return [T.cores[row * GC + c] for c in range(GC) if c != col]
+
+
+def _row_mask(T, topo, rank):
+    src = T.cores[rank]
+    m = topo.mask(src, _row_peers(T, rank)[0])
+    for d in _row_peers(T, rank):
+        m &= topo.mask(src, d)
+    return m
+
+
+def rank_program(g, core, T, topo):
+    rank = T.rank_of(core)
+    if rank is None:
+        return
+    row, col = rank // GC, rank % GC
+    S = T.sem
+    slot = T.ad[P * col:P * col + P, :]
+    partner_rank = (1 - row) * GC + col
+    partner = T.cores[partner_rank]
+
+    g.sync.dma_start(out=slot, in_=T.a[:, :]).then_inc(S.a_st, 16)
+    queues = [g.scalar, g.sync]
+    n = 0
+    for s in range(KB):
+        for t in range(KB):
+            k0 = (s - P * t) % KB
+            cnt = len(range(k0, P, KB))
+            p0 = (P * t + k0 - s) // KB
+            queues[n % 2].dma_start(out=T.bown[p0:p0 + cnt, F * s:F * s + F],
+                                    in_=T.b[k0:P:KB, F * t:F * t + F]).then_inc(S.b_ld, 16)
+            n += 1
+
+    peers = _row_peers(T, rank)
+    ma = _row_mask(T, topo, rank)
+    ids = []
+    for d in peers:
+        rid, pid = topo.addr(d, core)
+        ids.append(DstId(rid=rid, pnc=pid))
+    g.wait_ge(S.a_st, 16)
+    g.remote_dma_fused([RemoteDMATransfer(dst_ids=ids, dma_engine_mask=ma, remote_sem=S["a_in%d" % (col // KB)],
+                                          srcs=[slot], dsts=[slot for _ in peers], alu_op=0)],
+                       local_sem=S.sent)
+    mb = topo.mask(core, partner)
+    rid, pid = topo.addr(partner, core)
+    g.wait_ge(S.b_ld, 16 * NB)
+    g.remote_dma(out_ap=T.bpeer[:, :], in_ap=T.bown[:, :], remote_sem=S.b_in, local_sem=S.sent,
+                 pid=pid, routing_id=rid, dma_engine_mask=mb)
+
+    for h in range(GR):
+        q = (g.sync, g.scalar)[h]
+        need = sum(_engines(_row_mask(T, topo, row * GC + c)) for c in range(KB * h, KB * h + KB) if c != col)
+        if h == col // KB:
+            q.wait_ge(S.a_st, 16)
+        q.wait_ge(S["a_in%d" % h], need)
+        q.dma_start(out=T.asb[:, KB * P * h:KB * P * (h + 1)],
+                    in_=T.ad[KB * P * h:KB * P * (h + 1), :]).then_inc(S["a_sb%d" % h], 16)
+
+    te = g.tensor
+    acc = (T.acc0, T.acc1)
+    te.wait_ge(S.b_ld, 16 * NB)
+    te.wait_ge(S["a_sb%d" % row], 16)
+    for c in range(2):
+        for s in range(KB):
+            te.matmul(out=acc[c][:, 0:HF], lhsT=T.asb[:, (KB * row + s) * P:(KB * row + s + 1) * P],
+                      rhs=T.bown[:, F * s + HF * c:F * s + HF * c + HF], start=(s == 0), stop=False)
+    oth = 1 - row
+    te.wait_ge(S["a_sb%d" % oth], 16)
+    te.wait_ge(S.b_in, _engines(topo.mask(partner, core)))
+    for c in range(2):
+        for s in range(KB):
+            mm = te.matmul(out=acc[c][:, 0:HF], lhsT=T.asb[:, (KB * oth + s) * P:(KB * oth + s + 1) * P],
+                           rhs=T.bpeer[:, F * s + HF * c:F * s + HF * c + HF], start=False, stop=(s == KB - 1))
+            if s == KB - 1:
+                mm.then_inc(S["mm%d" % c], 1)
+
+    for c in range(2):
+        g.vector.wait_ge(S["mm%d" % c], 1)
+        g.vector.tensor_copy(out=T.ysb[:, HF * c:HF * c + HF], in_=acc[c][:, 0:HF]).then_inc(S["cp%d" % c], 1)
+    for c in range(2):
+        q = (g.sync, g.scalar)[c]
+        q.wait_ge(S["cp%d" % c], 1)
+        q.dma_start(out=T.y[:, HF * c:HF * c + HF], in_=T.ysb[:, HF * c:HF * c + HF]).then_inc(S["st%d" % c], 16)
+        q.wait_ge(S["st%d" % c], 16)
+
+    g.wait_ge(S.sent, _engines(ma) + _engines(mb))

@@ -2,10 +2,11 @@ from concourse.bass import DstId, RemoteDMATransfer
 
 GR, GC, KB, F, P = 2, 6, 3, 512, 128
 HF = F // 2
-NB = KB * KB
+CUT = KB * F - HF
+W = P // 2
 
 SCRATCH = {
-    "ad": ("dram", [GC * P, P], "bfloat16"),
+    "ad": ("dram", [GC * 2 * P, W], "bfloat16"),
     "asb": ("sbuf", [P, GC * P], "bfloat16"),
     "bown": ("sbuf", [P, KB * F], "bfloat16"),
     "bpeer": ("sbuf", [P, KB * F], "bfloat16"),
@@ -13,7 +14,7 @@ SCRATCH = {
     "acc0": ("psum", [P, F], "float32"),
     "acc1": ("psum", [P, F], "float32"),
 }
-SEMAPHORES = ["a_st", "b_ld", "a_in0", "a_in1", "a_sb0", "a_sb1", "b_in", "sent",
+SEMAPHORES = ["a_st0", "a_st1", "b_ld", "a_in0", "a_in1", "a_sb0", "a_sb1", "b_in0", "b_in1", "sent",
               "mm0", "mm1", "cp0", "cp1", "st0", "st1"]
 
 
@@ -21,9 +22,15 @@ def _engines(mask):
     return bin(mask).count("1")
 
 
+def _halves(mask):
+    bits = [b for b in range(16) if (mask >> b) & 1]
+    n = len(bits) // 2
+    return sum(1 << b for b in bits[:n]), sum(1 << b for b in bits[n:])
+
+
 def _row_peers(T, rank):
     row, col = rank // GC, rank % GC
-    return [T.cores[row * GC + c] for c in range(GC) if c != col]
+    return [T.cores[row * GC + (col + d) % GC] for d in range(1, GC)]
 
 
 def _row_mask(T, topo, rank):
@@ -39,12 +46,17 @@ def rank_program(g, core, T, topo):
     if rank is None:
         return
     row, col = rank // GC, rank % GC
+    oth = 1 - row
     S = T.sem
-    slot = T.ad[P * col:P * col + P, :]
-    partner_rank = (1 - row) * GC + col
-    partner = T.cores[partner_rank]
+    partner = T.cores[oth * GC + col]
+    piece = ((0, CUT), (CUT, KB * F))
+    ld = 16 * KB * KB
+    need = [sum(_engines(_row_mask(T, topo, row * GC + c)) for c in range(KB * h, KB * h + KB) if c != col)
+            for h in range(GR)]
+    halves = [T.ad[2 * P * col + P * u:2 * P * col + P * (u + 1), :] for u in range(2)]
 
-    g.sync.dma_start(out=slot, in_=T.a[:, :]).then_inc(S.a_st, 16)
+    for u, q in enumerate((g.sync, g.scalar)):
+        q.dma_start(out=halves[u], in_=T.a[W * u:W * (u + 1), :]).then_inc(S["a_st%d" % u], 16)
     queues = [g.scalar, g.sync]
     n = 0
     for s in range(KB):
@@ -56,44 +68,50 @@ def rank_program(g, core, T, topo):
                                     in_=T.b[k0:P:KB, F * t:F * t + F]).then_inc(S.b_ld, 16)
             n += 1
 
+    for h in (row, oth):
+        if h == col // KB:
+            for u in range(2):
+                g.sync.wait_ge(S["a_st%d" % u], 16)
+        g.sync.wait_ge(S["a_in%d" % h], need[h])
+        g.sync.dma_start(out=T.asb[:, KB * P * h:KB * P * (h + 1)],
+                         in_=T.ad[2 * KB * P * h:2 * KB * P * (h + 1), :]).then_inc(S["a_sb%d" % h], 16)
+
     peers = _row_peers(T, rank)
     ma = _row_mask(T, topo, rank)
     ids = []
     for d in peers:
         rid, pid = topo.addr(d, core)
         ids.append(DstId(rid=rid, pnc=pid))
-    g.wait_ge(S.a_st, 16)
-    g.remote_dma_fused([RemoteDMATransfer(dst_ids=ids, dma_engine_mask=ma, remote_sem=S["a_in%d" % (col // KB)],
-                                          srcs=[slot], dsts=[slot for _ in peers], alu_op=0)],
-                       local_sem=S.sent)
+    for u, m in enumerate(_halves(ma)):
+        g.wait_ge(S["a_st%d" % u], 16)
+        g.remote_dma_fused([RemoteDMATransfer(dst_ids=ids, dma_engine_mask=m, remote_sem=S["a_in%d" % (col // KB)],
+                                              srcs=[halves[u]], dsts=[halves[u] for _ in peers], alu_op=0)],
+                           local_sem=S.sent)
     mb = topo.mask(core, partner)
     rid, pid = topo.addr(partner, core)
-    g.wait_ge(S.b_ld, 16 * NB)
-    g.remote_dma(out_ap=T.bpeer[:, :], in_ap=T.bown[:, :], remote_sem=S.b_in, local_sem=S.sent,
-                 pid=pid, routing_id=rid, dma_engine_mask=mb)
-
-    for h in range(GR):
-        q = (g.sync, g.scalar)[h]
-        need = sum(_engines(_row_mask(T, topo, row * GC + c)) for c in range(KB * h, KB * h + KB) if c != col)
-        if h == col // KB:
-            q.wait_ge(S.a_st, 16)
-        q.wait_ge(S["a_in%d" % h], need)
-        q.dma_start(out=T.asb[:, KB * P * h:KB * P * (h + 1)],
-                    in_=T.ad[KB * P * h:KB * P * (h + 1), :]).then_inc(S["a_sb%d" % h], 16)
+    g.wait_ge(S.b_ld, ld)
+    for i, (lo, hi) in enumerate(piece):
+        if i == 1:
+            for h in range(GR):
+                g.wait_ge(S["a_in%d" % h], need[h])
+        g.remote_dma(out_ap=T.bpeer[:, lo:hi], in_ap=T.bown[:, lo:hi], remote_sem=S["b_in%d" % i],
+                     local_sem=S.sent, pid=pid, routing_id=rid, dma_engine_mask=mb)
 
     te = g.tensor
     acc = (T.acc0, T.acc1)
-    te.wait_ge(S.b_ld, 16 * NB)
+    nb = _engines(topo.mask(partner, core))
+    te.wait_ge(S.b_ld, ld)
     te.wait_ge(S["a_sb%d" % row], 16)
     for c in range(2):
         for s in range(KB):
             te.matmul(out=acc[c][:, 0:HF], lhsT=T.asb[:, (KB * row + s) * P:(KB * row + s + 1) * P],
                       rhs=T.bown[:, F * s + HF * c:F * s + HF * c + HF], start=(s == 0), stop=False)
-    oth = 1 - row
     te.wait_ge(S["a_sb%d" % oth], 16)
-    te.wait_ge(S.b_in, _engines(topo.mask(partner, core)))
+    te.wait_ge(S.b_in0, nb)
     for c in range(2):
         for s in range(KB):
+            if F * s + HF * c >= CUT:
+                te.wait_ge(S.b_in1, nb)
             mm = te.matmul(out=acc[c][:, 0:HF], lhsT=T.asb[:, (KB * oth + s) * P:(KB * oth + s + 1) * P],
                            rhs=T.bpeer[:, F * s + HF * c:F * s + HF * c + HF], start=False, stop=(s == KB - 1))
             if s == KB - 1:
@@ -108,4 +126,4 @@ def rank_program(g, core, T, topo):
         q.dma_start(out=T.y[:, HF * c:HF * c + HF], in_=T.ysb[:, HF * c:HF * c + HF]).then_inc(S["st%d" % c], 16)
         q.wait_ge(S["st%d" % c], 16)
 
-    g.wait_ge(S.sent, _engines(ma) + _engines(mb))
+    g.wait_ge(S.sent, _engines(ma) + 2 * _engines(mb))

from concourse.bass import DstId, RemoteDMATransfer

GR, GC, KB, F, P = 2, 6, 3, 512, 128
HF = F // 2
CUT = KB * F - HF
W = P // 2

SCRATCH = {
    "ad": ("dram", [GC * 2 * P, W], "bfloat16"),
    "asb": ("sbuf", [P, GC * P], "bfloat16"),
    "bown": ("sbuf", [P, KB * F], "bfloat16"),
    "bpeer": ("sbuf", [P, KB * F], "bfloat16"),
    "ysb": ("sbuf", [P, F], "bfloat16"),
    "acc0": ("psum", [P, F], "float32"),
    "acc1": ("psum", [P, F], "float32"),
}
SEMAPHORES = ["a_st0", "a_st1", "b_ld", "a_in0", "a_in1", "a_sb0", "a_sb1", "b_in0", "b_in1", "sent",
              "mm0", "mm1", "cp0", "cp1", "st0", "st1"]


def _engines(mask):
    return bin(mask).count("1")


def _halves(mask):
    bits = [b for b in range(16) if (mask >> b) & 1]
    n = len(bits) // 2
    return sum(1 << b for b in bits[:n]), sum(1 << b for b in bits[n:])


def _row_peers(T, rank):
    row, col = rank // GC, rank % GC
    return [T.cores[row * GC + (col + d) % GC] for d in range(1, GC)]


def _row_mask(T, topo, rank):
    src = T.cores[rank]
    m = topo.mask(src, _row_peers(T, rank)[0])
    for d in _row_peers(T, rank):
        m &= topo.mask(src, d)
    return m


def rank_program(g, core, T, topo):
    rank = T.rank_of(core)
    if rank is None:
        return
    row, col = rank // GC, rank % GC
    oth = 1 - row
    S = T.sem
    partner = T.cores[oth * GC + col]
    piece = ((0, CUT), (CUT, KB * F))
    ld = 16 * KB * KB
    need = [sum(_engines(_row_mask(T, topo, row * GC + c)) for c in range(KB * h, KB * h + KB) if c != col)
            for h in range(GR)]
    halves = [T.ad[2 * P * col + P * u:2 * P * col + P * (u + 1), :] for u in range(2)]

    for u, q in enumerate((g.sync, g.scalar)):
        q.dma_start(out=halves[u], in_=T.a[W * u:W * (u + 1), :]).then_inc(S["a_st%d" % u], 16)
    queues = [g.scalar, g.sync]
    n = 0
    for s in range(KB):
        for t in range(KB):
            k0 = (s - P * t) % KB
            cnt = len(range(k0, P, KB))
            p0 = (P * t + k0 - s) // KB
            queues[n % 2].dma_start(out=T.bown[p0:p0 + cnt, F * s:F * s + F],
                                    in_=T.b[k0:P:KB, F * t:F * t + F]).then_inc(S.b_ld, 16)
            n += 1

    for h in (row, oth):
        if h == col // KB:
            for u in range(2):
                g.sync.wait_ge(S["a_st%d" % u], 16)
        g.sync.wait_ge(S["a_in%d" % h], need[h])
        g.sync.dma_start(out=T.asb[:, KB * P * h:KB * P * (h + 1)],
                         in_=T.ad[2 * KB * P * h:2 * KB * P * (h + 1), :]).then_inc(S["a_sb%d" % h], 16)

    peers = _row_peers(T, rank)
    ma = _row_mask(T, topo, rank)
    ids = []
    for d in peers:
        rid, pid = topo.addr(d, core)
        ids.append(DstId(rid=rid, pnc=pid))
    for u, m in enumerate(_halves(ma)):
        g.wait_ge(S["a_st%d" % u], 16)
        g.remote_dma_fused([RemoteDMATransfer(dst_ids=ids, dma_engine_mask=m, remote_sem=S["a_in%d" % (col // KB)],
                                              srcs=[halves[u]], dsts=[halves[u] for _ in peers], alu_op=0)],
                           local_sem=S.sent)
    mb = topo.mask(core, partner)
    rid, pid = topo.addr(partner, core)
    g.wait_ge(S.b_ld, ld)
    for i, (lo, hi) in enumerate(piece):
        if i == 1:
            for h in range(GR):
                g.wait_ge(S["a_in%d" % h], need[h])
        g.remote_dma(out_ap=T.bpeer[:, lo:hi], in_ap=T.bown[:, lo:hi], remote_sem=S["b_in%d" % i],
                     local_sem=S.sent, pid=pid, routing_id=rid, dma_engine_mask=mb)

    te = g.tensor
    acc = (T.acc0, T.acc1)
    nb = _engines(topo.mask(partner, core))
    te.wait_ge(S.b_ld, ld)
    te.wait_ge(S["a_sb%d" % row], 16)
    for c in range(2):
        for s in range(KB):
            te.matmul(out=acc[c][:, 0:HF], lhsT=T.asb[:, (KB * row + s) * P:(KB * row + s + 1) * P],
                      rhs=T.bown[:, F * s + HF * c:F * s + HF * c + HF], start=(s == 0), stop=False)
    te.wait_ge(S["a_sb%d" % oth], 16)
    te.wait_ge(S.b_in0, nb)
    for c in range(2):
        for s in range(KB):
            if F * s + HF * c >= CUT:
                te.wait_ge(S.b_in1, nb)
            mm = te.matmul(out=acc[c][:, 0:HF], lhsT=T.asb[:, (KB * oth + s) * P:(KB * oth + s + 1) * P],
                           rhs=T.bpeer[:, F * s + HF * c:F * s + HF * c + HF], start=False, stop=(s == KB - 1))
            if s == KB - 1:
                mm.then_inc(S["mm%d" % c], 1)

    for c in range(2):
        g.vector.wait_ge(S["mm%d" % c], 1)
        g.vector.tensor_copy(out=T.ysb[:, HF * c:HF * c + HF], in_=acc[c][:, 0:HF]).then_inc(S["cp%d" % c], 1)
    for c in range(2):
        q = (g.sync, g.scalar)[c]
        q.wait_ge(S["cp%d" % c], 1)
        q.dma_start(out=T.y[:, HF * c:HF * c + HF], in_=T.ysb[:, HF * c:HF * c + HF]).then_inc(S["st%d" % c], 16)
        q.wait_ge(S["st%d" % c], 16)

    g.wait_ge(S.sent, _engines(ma) + 2 * _engines(mb))
